import numpy as np
import ml_dtypes


def mxq(x, axis, fmt="e4m3"):
    dtype, down = {"e4m3": (ml_dtypes.float8_e4m3fn, 7), "e5m2": (ml_dtypes.float8_e5m2, 14)}[fmt]
    v = np.moveaxis(np.asarray(x, np.float32).astype(ml_dtypes.bfloat16).astype(np.float64), axis, -1)
    blocks = v.reshape(v.shape[:-1] + (-1, 32))
    amax = np.abs(blocks).max(-1, keepdims=True)
    byte = np.maximum(np.where(amax > 0, np.frexp(amax)[1] - 1 + 127, 0) - down, 1)
    scale = np.exp2(byte - 127.0)
    codes = (blocks / scale).astype(np.float32).astype(dtype).astype(np.float64)
    return np.moveaxis((codes * scale).reshape(v.shape), -1, axis)


WIDE = False


def mx_kscale(k):
    if not WIDE:
        return np.ones(k)
    levels = np.array([10, -10, 5, -5, 0])
    if k % 512:
        return np.exp2(np.random.permutation(np.resize(levels, k // 32))).repeat(32)
    a = np.empty((k // 512, 16))
    for p in range(k // 512):
        a[p, :8] = np.random.permutation(np.resize(levels, 8))
        for g in range(8):
            far = levels[np.abs(levels - a[p, g]) >= 10]
            a[p, g + 8] = far[np.random.randint(len(far))]
    return np.exp2(a.ravel()).repeat(32)


def f64(x):
    return np.asarray(x).astype(np.float64)


def striped(idx):
    return np.tile(idx.reshape(-1, 16).T, (8, 1)).astype(np.uint16)


def unstriped(offs):
    return offs[:16].T.reshape(-1).astype(np.int64)


E2M1 = np.array([0.0, 0.5, 1.0, 1.5, 2.0, 3.0, 4.0, 6.0, -0.0, -0.5, -1.0, -1.5, -2.0, -3.0, -4.0, -6.0])


def pack_weight(w, fmt):
    k, n = w.shape
    w = f64(np.asarray(w, np.float32).astype(ml_dtypes.bfloat16)).reshape(k // 32, 32, n)
    amax = np.abs(w).max(1)
    if fmt == "e4m3":
        byte = np.frexp(amax)[1] - 1 + 127 - 7
    else:
        mant, ex = np.frexp(amax / 6.0)
        byte = np.where(mant > 0.5, ex, ex - 1) + 127
    byte = np.clip(np.where(amax > 0, byte, 1), 1, 254)
    scaled = (w * np.exp2(127.0 - byte)[:, None, :]).reshape(k, n).astype(np.float32)
    by_word = np.ascontiguousarray(scaled.reshape(k // 512, 128, 4, n).transpose(0, 1, 3, 2))
    if fmt == "e4m3":
        words = by_word.astype(ml_dtypes.float8_e4m3fn).view(np.uint8)
    else:
        c = by_word.astype(ml_dtypes.float4_e2m1fn).view(np.uint8) & 0xF
        words = (c[..., 0::2] | (c[..., 1::2] << 4)).reshape(k // 512, 128, 2 * n)
    return np.ascontiguousarray(words), np.ascontiguousarray(byte.astype(np.uint8).reshape(k // 512, 16, n))


def unpack_weight(words, scales, fmt):
    g, _, n = scales.shape
    words = np.ascontiguousarray(words).reshape(g, 128, n, -1)
    if fmt == "e4m3":
        vals = words.view(ml_dtypes.float8_e4m3fn).astype(np.float64)
    else:
        nib = np.empty((g, 128, n, 4), np.uint8)
        nib[..., 0::2] = words & 0xF
        nib[..., 1::2] = words >> 4
        vals = E2M1[nib]
    vals = vals * np.repeat(np.exp2(scales.astype(np.float64) - 127.0), 8, axis=1)[..., None]
    return vals.transpose(0, 1, 3, 2).reshape(g * 512, n)


def gelu(v):
    return 0.5 * v * (1.0 + np.tanh(np.sqrt(2.0 / np.pi) * (v + 0.044715 * v**3)))


K, H, T, S, T3, S2, P = 1024, 1024, 4096, 1024, 2048, 512, 512

def setup_inputs():
    n = np.random.standard_normal
    s = mx_kscale(K)[:, None]
    u = mx_kscale(H)[:, None]
    tab_words, tab_scales = pack_weight(n((K, T)) * s, "e4m3")
    tab2_words, tab2_scales = pack_weight(n((H, T3)) / np.sqrt(H) / u, "e4m3")
    return {
        "tab_words": tab_words, "tab_scales": tab_scales,
        "offs": striped(np.random.permutation(T)[:S]),
        "tab2_words": tab2_words, "tab2_scales": tab2_scales,
        "offs2": striped(np.random.permutation(T3)[:S2]),
        "pos1": striped(np.random.permutation(S)[:P]),
        "pos2": striped(np.random.permutation(S)[:P]),
        "w1": (1.5 * n((K, H)) / np.sqrt(K) / s).astype(np.float32),
        "b1": (0.6 * n(H)).astype(np.float32),
        "gain": (np.exp(0.4 * n(H)) * u[:, 0]).astype(np.float32),
        "prop": np.exp(0.4 * n(S2)).astype(np.float32),
    }

def reference(tab_words, tab_scales, offs, tab2_words, tab2_scales, offs2, pos1, pos2, w1, b1, gain, prop):
    v = unpack_weight(tab_words, tab_scales, "e4m3")[:, unstriped(offs)]
    v2 = unpack_weight(tab2_words, tab2_scales, "e4m3")[:, unstriped(offs2)]
    w1q = mxq(f64(w1), 0, "e4m3")
    h = f64(gain)[:, None] * np.tanh((w1q.T @ v) + f64(b1)[:, None])
    x1 = mxq(h[:, unstriped(pos1)], 0, "e4m3")
    x2 = mxq(np.abs(h[:, unstriped(pos2)]), 0, "e4m3")
    e1 = v2.T @ x1
    e2 = v2.T @ x2
    return f64(prop)[:, None] * e1 + e2

@@ -1,0 +1,263 @@
+from contextlib import ExitStack
+
+import concourse.mybir as mybir
+
+F32 = mybir.dt.float32
+BF16 = mybir.dt.bfloat16
+I32 = mybir.dt.int32
+U32 = mybir.dt.uint32
+U16 = mybir.dt.uint16
+U8 = mybir.dt.uint8
+FP8X4 = mybir.dt.float8_e4m3fn_x4
+ACT = mybir.ActivationFunctionType
+ALU = mybir.AluOpType
+
+P = 128
+PACK = 4
+K_PASS = P * PACK
+BANK = 512
+K, H, T, S, T3, S2, NP = 1024, 1024, 4096, 1024, 2048, 512, 512
+FLOPS = 2 * K * H * S + 2 * 2 * H * S2 * NP
+GAIN = "vector"
+LAST_GATHER = [512, 512]
+TAIL = [256, 128, 128]
+
+
+def tile_list_window_outfit_scorer_kernel(
+    tc, tab_words, tab_scales, offs, tab2_words, tab2_scales, offs2, pos1, pos2, w1, b1, gain, prop, out
+):
+    nc = tc.nc
+    with ExitStack() as ctx:
+        lists = ctx.enter_context(tc.tile_pool(name="lists", bufs=1))
+        keep = ctx.enter_context(tc.tile_pool(name="keep", bufs=1))
+        ring = ctx.enter_context(tc.tile_pool(name="ring", bufs=2))
+        psum = ctx.enter_context(tc.psum_pool(name="psum", bufs=1))
+
+        def load_list(src, name):
+            tile = lists.tile([P, src.shape[1]], U16, name=name)
+            nc.sync.dma_start(tile[:], src)
+            return tile
+
+        def load_words(words, a, name):
+            tile = keep.tile([P, words.shape[2]], I32, name=name)
+            nc.sync.dma_start(tile[:], words[a].rearrange("p n i -> p (n i)").bitcast(I32))
+            return tile
+
+        def load_scales(scales, name, queue):
+            tile = keep.tile([P, scales.shape[2]], U8, name=name, tag=name, align_bytes=64)
+            nc.vector.memset(tile[:].bitcast(I32), 0)
+            for q in range(4):
+                queue.dma_start(
+                    tile[32 * q : 32 * q + 8, :].bitcast(I32), scales[:, 4 * q : 4 * q + 4, :].bitcast(I32)
+                )
+            return tile
+
+        def load_w1(a, b):
+            tile = keep.tile([P, PACK, K_PASS], F32, name=f"w_raw{a}{b}")
+            src = w1[K_PASS * a : K_PASS * (a + 1), K_PASS * b : K_PASS * (b + 1)]
+            nc.sync.dma_start(tile[:], src.rearrange("(p j) c -> p j c", j=PACK))
+            return tile
+
+        def round_w1(raw, on_vector, slot):
+            tile = keep.tile([P, PACK, P, PACK], BF16, name="w_bf", tag=slot, align_bytes=64)
+            dst = tile[:].rearrange("p t m j -> p m j t")
+            src = raw[:].rearrange("p j (m t) -> p m j t", t=PACK)
+            if on_vector:
+                nc.vector.tensor_copy(dst, src)
+            else:
+                nc.scalar.activation(dst, src, ACT.Copy)
+            return tile[:].rearrange("p t m j -> p (t m j)")
+
+        def quantize(values, name, slots=None):
+            width = values.shape[1] // PACK
+            slots = slots or (name + "_codes", name + "_scales")
+            codes = keep.tile([P, width], U32, name=name + "_codes", tag=slots[0], align_bytes=64)
+            scales = keep.tile([P, width], U8, name=name + "_scales", tag=slots[1], align_bytes=64)
+            nc.vector.quantize_mx(out=codes[:].bitcast(FP8X4), scales=scales[:], in_=values)
+            return codes, scales
+
+        def gather(dst, window, offsets, lo, hi):
+            nc.vector.tensor_copy(dst, window.indirect(offsets[:, lo // 16 : hi // 16]))
+
+        def bank(i, shape):
+            return psum.tile(shape, F32, name=f"bank{i}")
+
+        offs_t = load_list(offs, "offs_t")
+        tab_sc = load_scales(tab_scales, "tab_sc", nc.gpsimd)
+        w_raw = {}
+        w_raw[0, 0] = load_w1(0, 0)
+        w_raw[1, 0] = load_w1(1, 0)
+        tab_w = [load_words(tab_words, a, f"tab_w{a}") for a in range(2)]
+        b1_t = keep.tile([P, 2, PACK], F32, name="b1_t")
+        gain_t = keep.tile([P, 2, PACK], F32, name="gain_t")
+        nc.scalar.dma_start(b1_t[:], b1.rearrange("(b p t) -> p b t", b=2, t=PACK))
+        nc.scalar.dma_start(gain_t[:], gain.rearrange("(b p t) -> p b t", b=2, t=PACK))
+        pos1_t = load_list(pos1, "pos1_t")
+        pos2_t = load_list(pos2, "pos2_t")
+        offs2_t = load_list(offs2, "offs2_t")
+        tab2_sc = load_scales(tab2_scales, "tab2_sc", nc.sync)
+        w_raw[0, 1] = load_w1(0, 1)
+        w_raw[1, 1] = load_w1(1, 1)
+        tab2_w = [load_words(tab2_words, b, f"tab2_w{b}") for b in range(2)]
+        prop_t = keep.tile([P, S2 // P], F32, name="prop_t")
+        with nc.allow_non_contiguous_dma(reason="one value of prop for each output row"):
+            nc.sync.dma_start(prop_t[:], prop.rearrange("(j p) -> p j", p=P))
+
+        wq = {}
+        wq[0, 0] = quantize(round_w1(w_raw[0, 0], True, "slot_a"), "wq00")
+        wq[1, 0] = quantize(round_w1(w_raw[1, 0], True, "slot_b"), "wq10", ("slot_c", "slot_d"))
+
+        gain_rows = {}
+        if GAIN == "fused":
+            for b in range(2):
+                for t in range(PACK):
+                    gain_rows[b, t] = keep.tile([P, NP], F32, name=f"gain_rows{b}{t}")
+                    nc.scalar.activation(gain_rows[b, t][:], gain_t[:, b, t : t + 1].to_broadcast([P, NP]), ACT.Copy)
+
+        v_sc = keep.tile([P, S], U8, name="v_sc", align_bytes=64)
+        gather(v_sc[:], tab_sc[:], offs_t, 0, S)
+        v_w = [keep.tile([P, S], U32, name=f"v_w{a}", tag=("tab_sc", "v_w1")[a], align_bytes=64) for a in range(2)]
+        gather(v_w[0][:], tab_w[0][:].bitcast(U32), offs_t, 0, S)
+        lo = 0
+        for width in LAST_GATHER:
+            gather(v_w[1][:, lo : lo + width], tab_w[1][:].bitcast(U32), offs_t, lo, lo + width)
+            lo += width
+
+        def first_stage(b, t, widths):
+            tanh_t = ring.tile([P, S], F32, name="tanh_t", bufs=3) if GAIN != "fused" else None
+            h = keep.tile([P, S], F32, name=f"h{b}{t}")
+            banks = [bank(2 * t + half, [P, BANK]) for half in range(2)]
+            pieces = []
+            lo = 0
+            for width in widths:
+                pieces.append((lo, lo + width))
+                lo += width
+            for a in range(2):
+                codes, scales = wq[a, b]
+                for lo, hi in [(0, BANK), (BANK, S)] if a == 0 else pieces:
+                    nc.tensor.matmul_mx(
+                        out=banks[lo // BANK][:, lo % BANK : lo % BANK + hi - lo],
+                        lhsT=codes[:, P * t : P * (t + 1)].bitcast(FP8X4),
+                        lhsT_scale=scales[:, P * t : P * (t + 1)],
+                        rhs=v_w[a][:, lo:hi].bitcast(FP8X4),
+                        rhs_scale=v_sc[4 * a : P, lo:hi],
+                        start=(a == 0),
+                        stop=(a == 1 and hi % BANK == 0),
+                    )
+            for half in range(2):
+                cols = slice(BANK * half, BANK * (half + 1))
+                dst = h if GAIN == "fused" else tanh_t
+                nc.scalar.activation(dst[:, cols], banks[half][:], ACT.Tanh, bias=b1_t[:, b, t : t + 1])
+            g = gain_t[:, b, t : t + 1]
+            if GAIN == "vector" or (GAIN == "gpsimd" and (b, t) == (0, 0)):
+                if (b, t) == (0, 0):
+                    for half in range(2):
+                        cols = slice(BANK * half, BANK * (half + 1))
+                        nc.vector.tensor_scalar(h[:, cols], tanh_t[:, cols], g, None, ALU.mult)
+                else:
+                    nc.vector.tensor_scalar(h[:], tanh_t[:], g, None, ALU.mult)
+            elif GAIN == "gpsimd":
+                nc.gpsimd.tensor_scalar(h[:], tanh_t[:], g, 0.0, ALU.mult, ALU.add)
+            return h
+
+        def pick(dst, b, t, h, offsets, lo, hi):
+            if GAIN == "fused":
+                nc.vector.tensor_tensor(
+                    dst, h[:].indirect(offsets[:, lo // 16 : hi // 16]), gain_rows[b, t][:, 0 : hi - lo], ALU.mult
+                )
+            else:
+                gather(dst, h[:], offsets, lo, hi)
+
+        def round_x(picked, func, slot):
+            width = picked.shape[2]
+            tile = keep.tile([P, width, PACK], BF16, name="x_bf", tag=slot, align_bytes=64)
+            nc.scalar.activation(
+                tile[:].rearrange("p (c i) t -> p c t i", i=4),
+                picked[:].rearrange("p t (c i) -> p c t i", i=4),
+                func,
+            )
+            return tile[:].rearrange("p n t -> p (n t)")
+
+        h = {}
+        for t in range(PACK):
+            h[0, t] = first_stage(0, t, LAST_GATHER if t == 0 else [BANK, BANK])
+
+        v2_sc = keep.tile([P, S2], U8, name="v2_sc", align_bytes=64)
+        gather(v2_sc[:], tab2_sc[:], offs2_t, 0, S2)
+
+        lead = keep.tile([P, PACK, NP], F32, name="lead0", tag="slot_e", align_bytes=64)
+        for t in range(PACK):
+            pick(lead[:, t, :], 0, t, h[0, t], pos1_t, 0, NP)
+        wq[0, 1] = quantize(round_w1(w_raw[0, 1], False, "slot_c"), "wq01")
+        wq[1, 1] = quantize(round_w1(w_raw[1, 1], False, "slot_d"), "wq11", ("slot_a", "slot_b"))
+        accent = keep.tile([P, PACK, NP], F32, name="accent0", tag="slot_c", align_bytes=64)
+        for t in range(PACK):
+            pick(accent[:, t, :], 0, t, h[0, t], pos2_t, 0, NP)
+        for t in range(PACK):
+            h[1, t] = first_stage(1, t, [BANK, BANK])
+
+        v2_w = [keep.tile([P, S2], U32, name=f"v2_w{b}", align_bytes=64) for b in range(2)]
+        for b in range(2):
+            gather(v2_w[b][:], tab2_w[b][:].bitcast(U32), offs2_t, 0, S2)
+
+        x1_bf0 = round_x(lead, ACT.Copy, "slot_a")
+        x2_bf0 = round_x(accent, ACT.Abs, "slot_b")
+        lead = keep.tile([P, PACK, NP], F32, name="lead1", tag="slot_f", align_bytes=64)
+        for t in range(PACK):
+            pick(lead[:, t, :], 1, t, h[1, t], pos1_t, 0, NP)
+            if t == 1:
+                x1q0 = quantize(x1_bf0, "x1q0")
+            if t == 3:
+                x2q0 = quantize(x2_bf0, "x2q0")
+        x1_bf1 = round_x(lead, ACT.Copy, "slot_g")
+
+        def second_stage(dst, b, j, xq, lo, hi, start, stop):
+            codes, scales = xq
+            nc.tensor.matmul_mx(
+                out=dst,
+                lhsT=v2_w[b][:, P * j : P * (j + 1)].bitcast(FP8X4),
+                lhsT_scale=v2_sc[4 * b : P, P * j : P * (j + 1)],
+                rhs=codes[:, lo:hi].bitcast(FP8X4),
+                rhs_scale=scales[:, lo:hi],
+                start=start,
+                stop=stop,
+            )
+
+        e1 = [bank(j, [P, NP]) for j in range(4)]
+        for j in range(4):
+            second_stage(e1[j][:], 0, j, x1q0, 0, NP, True, False)
+        e2 = []
+        lo = 0
+        nbank = 4
+        for width in TAIL:
+            per = BANK // width
+            for j0 in range(0, 4, per):
+                tile = bank(nbank, [P, per, width])
+                nbank += 1
+                for i in range(per):
+                    second_stage(tile[:, i, :], 0, j0 + i, x2q0, lo, lo + width, i == 0, False)
+                e2.append((tile, j0, per, lo, width))
+            lo += width
+
+        weighed = keep.tile([P, 4, NP], F32, name="weighed")
+        out_v = out.rearrange("(j p) n -> p j n", p=P)
+        lo = 0
+        for s, width in enumerate(TAIL):
+            accent = keep.tile([P, PACK, width], F32, name="accent1", tag=("slot_e", "slot_f", "slot_g")[s], align_bytes=64)
+            for t in range(PACK):
+                pick(accent[:, t, :], 1, t, h[1, t], pos2_t, lo, lo + width)
+                if s == 0 and t == 2:
+                    x1q1 = quantize(x1_bf1, "x1q1")
+                    for j in range(4):
+                        second_stage(e1[j][:], 1, j, x1q1, 0, NP, False, True)
+                        nc.scalar.activation(weighed[:, j, :], e1[j][:], ACT.Copy, scale=prop_t[:, j : j + 1])
+            xq = quantize(round_x(accent, ACT.Abs, f"x2_bf1{s}"), f"x2q1{s}")
+            for tile, j0, per, lo2, width2 in e2:
+                if lo2 == lo:
+                    for i in range(per):
+                        second_stage(tile[:, i, :], 1, j0 + i, xq, 0, width, False, i == per - 1)
+            lo += width
+        for tile, j0, per, lo, width in e2:
+            res = ring.tile([P, per, width], F32, name="res", bufs=4)
+            nc.vector.tensor_tensor(res[:], tile[:], weighed[:, j0 : j0 + per, lo : lo + width], ALU.add)
+            nc.sync.dma_start(out_v[:, j0 : j0 + per, lo : lo + width], res[:])

@@ -18,7 +18,7 @@ K_PASS = P * PACK
 BANK = 512
 K, H, T, S, T3, S2, NP = 1024, 1024, 4096, 1024, 2048, 512, 512
 FLOPS = 2 * K * H * S + 2 * 2 * H * S2 * NP
-GAIN = "vector"
+GAIN = "fused"
 LAST_GATHER = [512, 512]
 TAIL = [256, 128, 128]
 
@@ -188,9 +188,9 @@ def tile_list_window_outfit_scorer_kernel(
         lead = keep.tile([P, PACK, NP], F32, name="lead0", tag="slot_e", align_bytes=64)
         for t in range(PACK):
             pick(lead[:, t, :], 0, t, h[0, t], pos1_t, 0, NP)
-        wq[0, 1] = quantize(round_w1(w_raw[0, 1], False, "slot_c"), "wq01")
+        wq[0, 1] = quantize(round_w1(w_raw[0, 1], True, "slot_c"), "wq01")
         wq[1, 1] = quantize(round_w1(w_raw[1, 1], False, "slot_d"), "wq11", ("slot_a", "slot_b"))
-        accent = keep.tile([P, PACK, NP], F32, name="accent0", tag="slot_c", align_bytes=64)
+        accent = keep.tile([P, PACK, NP], F32, name="accent0", tag="slot_d", align_bytes=64)
         for t in range(PACK):
             pick(accent[:, t, :], 0, t, h[0, t], pos2_t, 0, NP)
         for t in range(PACK):

@@ -39,7 +39,7 @@ def tile_list_window_outfit_scorer_kernel(
             return tile
 
         def load_words(words, a, name):
-            tile = keep.tile([P, words.shape[2]], I32, name=name)
+            tile = keep.tile([P, words.shape[2]], I32, name=name, tag=name, align_bytes=64)
             nc.sync.dma_start(tile[:], words[a].rearrange("p n i -> p (n i)").bitcast(I32))
             return tile
 
@@ -82,26 +82,42 @@ def tile_list_window_outfit_scorer_kernel(
         def bank(i, shape):
             return psum.tile(shape, F32, name=f"bank{i}")
 
-        offs_t = load_list(offs, "offs_t")
-        tab_sc = load_scales(tab_scales, "tab_sc", nc.gpsimd)
+        landed = keep.tile([P, T], U8, name="landed", align_bytes=64)
+
+        def load_scale_rows(a, q):
+            row = 32 * q + 4 * a
+            nc.sync.dma_start(landed[row : row + 4, :].bitcast(I32), tab_scales[a, 4 * q : 4 * q + 4, :].bitcast(I32))
+
+        runs = [(a, q) for q in range(4) for a in range(2)]
+        for a, q in runs[:7]:
+            load_scale_rows(a, q)
         w_raw = {}
         w_raw[0, 0] = load_w1(0, 0)
-        w_raw[1, 0] = load_w1(1, 0)
-        tab_w = [load_words(tab_words, a, f"tab_w{a}") for a in range(2)]
+        load_scale_rows(*runs[7])
+        offs_t = load_list(offs, "offs_t")
         b1_t = keep.tile([P, 2, PACK], F32, name="b1_t")
         gain_t = keep.tile([P, 2, PACK], F32, name="gain_t")
-        nc.scalar.dma_start(b1_t[:], b1.rearrange("(b p t) -> p b t", b=2, t=PACK))
-        nc.scalar.dma_start(gain_t[:], gain.rearrange("(b p t) -> p b t", b=2, t=PACK))
+        nc.sync.dma_start(gain_t[:], gain.rearrange("(b p t) -> p b t", b=2, t=PACK))
+        nc.sync.dma_start(b1_t[:], b1.rearrange("(b p t) -> p b t", b=2, t=PACK))
+        w_raw[1, 0] = load_w1(1, 0)
+        tab_w = [load_words(tab_words, 0, "tab_w0")]
         pos1_t = load_list(pos1, "pos1_t")
         pos2_t = load_list(pos2, "pos2_t")
-        offs2_t = load_list(offs2, "offs2_t")
-        tab2_sc = load_scales(tab2_scales, "tab2_sc", nc.sync)
+        tab_w.append(load_words(tab_words, 1, "tab_w1"))
         w_raw[0, 1] = load_w1(0, 1)
         w_raw[1, 1] = load_w1(1, 1)
-        tab2_w = [load_words(tab2_words, b, f"tab2_w{b}") for b in range(2)]
+        offs2_t = load_list(offs2, "offs2_t")
         prop_t = keep.tile([P, S2 // P], F32, name="prop_t")
         with nc.allow_non_contiguous_dma(reason="one value of prop for each output row"):
             nc.sync.dma_start(prop_t[:], prop.rearrange("(j p) -> p j", p=P))
+        tab2_sc = load_scales(tab2_scales, "tab2_sc", nc.sync)
+        tab2_w = [load_words(tab2_words, b, f"tab2_w{b}") for b in range(2)]
+
+        tab_sc = keep.tile([P, T], U8, name="tab_sc", tag="tab_sc", align_bytes=64)
+        nc.vector.memset(tab_sc[:].bitcast(I32), 0)
+        for q in range(4):
+            rows = slice(32 * q, 32 * q + 8)
+            nc.vector.tensor_copy(tab_sc[rows, :].bitcast(I32), landed[rows, :].bitcast(I32))
 
         wq = {}
         wq[0, 0] = quantize(round_w1(w_raw[0, 0], True, "slot_a"), "wq00")
@@ -182,13 +198,14 @@ def tile_list_window_outfit_scorer_kernel(
         for t in range(PACK):
             h[0, t] = first_stage(0, t, LAST_GATHER if t == 0 else [BANK, BANK])
 
-        v2_sc = keep.tile([P, S2], U8, name="v2_sc", align_bytes=64)
-        gather(v2_sc[:], tab2_sc[:], offs2_t, 0, S2)
+        w01_bf = round_w1(w_raw[0, 1], True, "tab_w1")
 
         lead = keep.tile([P, PACK, NP], F32, name="lead0", tag="slot_e", align_bytes=64)
         for t in range(PACK):
             pick(lead[:, t, :], 0, t, h[0, t], pos1_t, 0, NP)
-        wq[0, 1] = quantize(round_w1(w_raw[0, 1], True, "slot_c"), "wq01")
+        wq[0, 1] = quantize(w01_bf, "wq01")
+        v2_sc = keep.tile([P, S2], U8, name="v2_sc", align_bytes=64)
+        gather(v2_sc[:], tab2_sc[:], offs2_t, 0, S2)
         wq[1, 1] = quantize(round_w1(w_raw[1, 1], False, "slot_d"), "wq11", ("slot_a", "slot_b"))
         accent = keep.tile([P, PACK, NP], F32, name="accent0", tag="slot_d", align_bytes=64)
         for t in range(PACK):
@@ -200,7 +217,7 @@ def tile_list_window_outfit_scorer_kernel(
         for b in range(2):
             gather(v2_w[b][:], tab2_w[b][:].bitcast(U32), offs2_t, 0, S2)
 
-        x1_bf0 = round_x(lead, ACT.Copy, "slot_a")
+        x1_bf0 = round_x(lead, ACT.Copy, "slot_c")
         x2_bf0 = round_x(accent, ACT.Abs, "slot_b")
         lead = keep.tile([P, PACK, NP], F32, name="lead1", tag="slot_f", align_bytes=64)
         for t in range(PACK):

@@ -15,12 +15,14 @@ ALU = mybir.AluOpType
 P = 128
 PACK = 4
 K_PASS = P * PACK
+PASSES = 2
 BANK = 512
-K, H, T, S, T3, S2, NP = 1024, 1024, 4096, 1024, 2048, 512, 512
-FLOPS = 2 * K * H * S + 2 * 2 * H * S2 * NP
-GAIN = "fused"
-LAST_GATHER = [512, 512]
-TAIL = [256, 128, 128]
+K, H, T, S, S2, OUTFITS = 1024, 1024, 4096, 1024, 512, 512
+ROW_TILES = S2 // P
+FLOPS = 2 * K * H * S + 2 * 2 * H * S2 * OUTFITS
+
+FIRST_PIECES = [512, 256, 256]
+SLICE = 256
 
 
 def tile_list_window_outfit_scorer_kernel(
@@ -30,8 +32,13 @@ def tile_list_window_outfit_scorer_kernel(
     with ExitStack() as ctx:
         lists = ctx.enter_context(tc.tile_pool(name="lists", bufs=1))
         keep = ctx.enter_context(tc.tile_pool(name="keep", bufs=1))
-        ring = ctx.enter_context(tc.tile_pool(name="ring", bufs=2))
         psum = ctx.enter_context(tc.psum_pool(name="psum", bufs=1))
+
+        def sbuf(shape, dtype, name, tag=None):
+            return keep.tile(shape, dtype, name=name, tag=tag or name, align_bytes=64)
+
+        def bank(i, shape):
+            return psum.tile(shape, F32, name=f"bank{i}")
 
         def load_list(src, name):
             tile = lists.tile([P, src.shape[1]], U16, name=name)
@@ -39,27 +46,23 @@ def tile_list_window_outfit_scorer_kernel(
             return tile
 
         def load_words(words, a, name):
-            tile = keep.tile([P, words.shape[2]], I32, name=name, tag=name, align_bytes=64)
+            tile = sbuf([P, words.shape[2]], I32, name)
             nc.sync.dma_start(tile[:], words[a].rearrange("p n i -> p (n i)").bitcast(I32))
             return tile
 
-        def load_scales(scales, name, queue):
-            tile = keep.tile([P, scales.shape[2]], U8, name=name, tag=name, align_bytes=64)
-            nc.vector.memset(tile[:].bitcast(I32), 0)
-            for q in range(4):
-                queue.dma_start(
-                    tile[32 * q : 32 * q + 8, :].bitcast(I32), scales[:, 4 * q : 4 * q + 4, :].bitcast(I32)
-                )
-            return tile
-
         def load_w1(a, b):
-            tile = keep.tile([P, PACK, K_PASS], F32, name=f"w_raw{a}{b}")
+            tile = sbuf([P, PACK, K_PASS], F32, f"w_raw{a}{b}")
             src = w1[K_PASS * a : K_PASS * (a + 1), K_PASS * b : K_PASS * (b + 1)]
             nc.sync.dma_start(tile[:], src.rearrange("(p j) c -> p j c", j=PACK))
             return tile
 
-        def round_w1(raw, on_vector, slot):
-            tile = keep.tile([P, PACK, P, PACK], BF16, name="w_bf", tag=slot, align_bytes=64)
+        def load_per_row(vector, name):
+            tile = keep.tile([P, PASSES, PACK], F32, name=name)
+            nc.sync.dma_start(tile[:], vector.rearrange("(b p t) -> p b t", b=PASSES, t=PACK))
+            return tile
+
+        def round_w1(raw, on_vector, tag):
+            tile = sbuf([P, PACK, P, PACK], BF16, "w_bf", tag)
             dst = tile[:].rearrange("p t m j -> p m j t")
             src = raw[:].rearrange("p j (m t) -> p m j t", t=PACK)
             if on_vector:
@@ -68,125 +71,8 @@ def tile_list_window_outfit_scorer_kernel(
                 nc.scalar.activation(dst, src, ACT.Copy)
             return tile[:].rearrange("p t m j -> p (t m j)")
 
-        def quantize(values, name, slots=None):
-            width = values.shape[1] // PACK
-            slots = slots or (name + "_codes", name + "_scales")
-            codes = keep.tile([P, width], U32, name=name + "_codes", tag=slots[0], align_bytes=64)
-            scales = keep.tile([P, width], U8, name=name + "_scales", tag=slots[1], align_bytes=64)
-            nc.vector.quantize_mx(out=codes[:].bitcast(FP8X4), scales=scales[:], in_=values)
-            return codes, scales
-
-        def gather(dst, window, offsets, lo, hi):
-            nc.vector.tensor_copy(dst, window.indirect(offsets[:, lo // 16 : hi // 16]))
-
-        def bank(i, shape):
-            return psum.tile(shape, F32, name=f"bank{i}")
-
-        landed = keep.tile([P, T], U8, name="landed", align_bytes=64)
-
-        def load_scale_rows(a, q):
-            row = 32 * q + 4 * a
-            nc.sync.dma_start(landed[row : row + 4, :].bitcast(I32), tab_scales[a, 4 * q : 4 * q + 4, :].bitcast(I32))
-
-        runs = [(a, q) for q in range(4) for a in range(2)]
-        for a, q in runs[:7]:
-            load_scale_rows(a, q)
-        w_raw = {}
-        w_raw[0, 0] = load_w1(0, 0)
-        load_scale_rows(*runs[7])
-        offs_t = load_list(offs, "offs_t")
-        b1_t = keep.tile([P, 2, PACK], F32, name="b1_t")
-        gain_t = keep.tile([P, 2, PACK], F32, name="gain_t")
-        nc.sync.dma_start(gain_t[:], gain.rearrange("(b p t) -> p b t", b=2, t=PACK))
-        nc.sync.dma_start(b1_t[:], b1.rearrange("(b p t) -> p b t", b=2, t=PACK))
-        w_raw[1, 0] = load_w1(1, 0)
-        tab_w = [load_words(tab_words, 0, "tab_w0")]
-        pos1_t = load_list(pos1, "pos1_t")
-        pos2_t = load_list(pos2, "pos2_t")
-        tab_w.append(load_words(tab_words, 1, "tab_w1"))
-        w_raw[0, 1] = load_w1(0, 1)
-        w_raw[1, 1] = load_w1(1, 1)
-        offs2_t = load_list(offs2, "offs2_t")
-        prop_t = keep.tile([P, S2 // P], F32, name="prop_t")
-        with nc.allow_non_contiguous_dma(reason="one value of prop for each output row"):
-            nc.sync.dma_start(prop_t[:], prop.rearrange("(j p) -> p j", p=P))
-        tab2_sc = load_scales(tab2_scales, "tab2_sc", nc.sync)
-        tab2_w = [load_words(tab2_words, b, f"tab2_w{b}") for b in range(2)]
-
-        tab_sc = keep.tile([P, T], U8, name="tab_sc", tag="tab_sc", align_bytes=64)
-        nc.vector.memset(tab_sc[:].bitcast(I32), 0)
-        for q in range(4):
-            rows = slice(32 * q, 32 * q + 8)
-            nc.vector.tensor_copy(tab_sc[rows, :].bitcast(I32), landed[rows, :].bitcast(I32))
-
-        wq = {}
-        wq[0, 0] = quantize(round_w1(w_raw[0, 0], True, "slot_a"), "wq00")
-        wq[1, 0] = quantize(round_w1(w_raw[1, 0], True, "slot_b"), "wq10", ("slot_c", "slot_d"))
-
-        gain_rows = {}
-        if GAIN == "fused":
-            for b in range(2):
-                for t in range(PACK):
-                    gain_rows[b, t] = keep.tile([P, NP], F32, name=f"gain_rows{b}{t}")
-                    nc.scalar.activation(gain_rows[b, t][:], gain_t[:, b, t : t + 1].to_broadcast([P, NP]), ACT.Copy)
-
-        v_sc = keep.tile([P, S], U8, name="v_sc", align_bytes=64)
-        gather(v_sc[:], tab_sc[:], offs_t, 0, S)
-        v_w = [keep.tile([P, S], U32, name=f"v_w{a}", tag=("tab_sc", "v_w1")[a], align_bytes=64) for a in range(2)]
-        gather(v_w[0][:], tab_w[0][:].bitcast(U32), offs_t, 0, S)
-        lo = 0
-        for width in LAST_GATHER:
-            gather(v_w[1][:, lo : lo + width], tab_w[1][:].bitcast(U32), offs_t, lo, lo + width)
-            lo += width
-
-        def first_stage(b, t, widths):
-            tanh_t = ring.tile([P, S], F32, name="tanh_t", bufs=3) if GAIN != "fused" else None
-            h = keep.tile([P, S], F32, name=f"h{b}{t}")
-            banks = [bank(2 * t + half, [P, BANK]) for half in range(2)]
-            pieces = []
-            lo = 0
-            for width in widths:
-                pieces.append((lo, lo + width))
-                lo += width
-            for a in range(2):
-                codes, scales = wq[a, b]
-                for lo, hi in [(0, BANK), (BANK, S)] if a == 0 else pieces:
-                    nc.tensor.matmul_mx(
-                        out=banks[lo // BANK][:, lo % BANK : lo % BANK + hi - lo],
-                        lhsT=codes[:, P * t : P * (t + 1)].bitcast(FP8X4),
-                        lhsT_scale=scales[:, P * t : P * (t + 1)],
-                        rhs=v_w[a][:, lo:hi].bitcast(FP8X4),
-                        rhs_scale=v_sc[4 * a : P, lo:hi],
-                        start=(a == 0),
-                        stop=(a == 1 and hi % BANK == 0),
-                    )
-            for half in range(2):
-                cols = slice(BANK * half, BANK * (half + 1))
-                dst = h if GAIN == "fused" else tanh_t
-                nc.scalar.activation(dst[:, cols], banks[half][:], ACT.Tanh, bias=b1_t[:, b, t : t + 1])
-            g = gain_t[:, b, t : t + 1]
-            if GAIN == "vector" or (GAIN == "gpsimd" and (b, t) == (0, 0)):
-                if (b, t) == (0, 0):
-                    for half in range(2):
-                        cols = slice(BANK * half, BANK * (half + 1))
-                        nc.vector.tensor_scalar(h[:, cols], tanh_t[:, cols], g, None, ALU.mult)
-                else:
-                    nc.vector.tensor_scalar(h[:], tanh_t[:], g, None, ALU.mult)
-            elif GAIN == "gpsimd":
-                nc.gpsimd.tensor_scalar(h[:], tanh_t[:], g, 0.0, ALU.mult, ALU.add)
-            return h
-
-        def pick(dst, b, t, h, offsets, lo, hi):
-            if GAIN == "fused":
-                nc.vector.tensor_tensor(
-                    dst, h[:].indirect(offsets[:, lo // 16 : hi // 16]), gain_rows[b, t][:, 0 : hi - lo], ALU.mult
-                )
-            else:
-                gather(dst, h[:], offsets, lo, hi)
-
-        def round_x(picked, func, slot):
-            width = picked.shape[2]
-            tile = keep.tile([P, width, PACK], BF16, name="x_bf", tag=slot, align_bytes=64)
+        def round_x(picked, func, tag):
+            tile = sbuf([P, picked.shape[2], PACK], BF16, "x_bf", tag)
             nc.scalar.activation(
                 tile[:].rearrange("p (c i) t -> p c t i", i=4),
                 picked[:].rearrange("p t (c i) -> p c t i", i=4),
@@ -194,41 +80,147 @@ def tile_list_window_outfit_scorer_kernel(
             )
             return tile[:].rearrange("p n t -> p (n t)")
 
+        def quantize(values, name):
+            width = values.shape[1] // PACK
+            codes = sbuf([P, width], U32, name + "_codes")
+            scales = sbuf([P, width], U8, name + "_scales")
+            nc.vector.quantize_mx(out=codes[:].bitcast(FP8X4), scales=scales[:], in_=values)
+            return codes, scales
+
+        def looked_up(window, offsets, lo, hi):
+            return window.indirect(offsets[:, lo // 16 : hi // 16])
+
+        landed = sbuf([P, T], U8, "landed")
+
+        def load_scale_rows(a, q):
+            row = 32 * q + 4 * a
+            nc.sync.dma_start(landed[row : row + 4, :].bitcast(I32), tab_scales[a, 4 * q : 4 * q + 4, :].bitcast(I32))
+
+        runs = [(a, q) for q in range(4) for a in range(PASSES)]
+        for a, q in runs[:-1]:
+            load_scale_rows(a, q)
+        w_raw = {(0, 0): load_w1(0, 0)}
+        load_scale_rows(*runs[-1])
+        offs_t = load_list(offs, "offs_t")
+        gain_t = load_per_row(gain, "gain_t")
+        b1_t = load_per_row(b1, "b1_t")
+        w_raw[1, 0] = load_w1(1, 0)
+        tab_w = [load_words(tab_words, a, f"tab_w{a}") for a in range(PASSES)]
+        offs2_t = load_list(offs2, "offs2_t")
+        tab2_sc = sbuf([P, tab2_scales.shape[2]], U8, "tab2_sc")
+        nc.vector.memset(tab2_sc[:].bitcast(I32), 0)
+        for q in range(4):
+            nc.sync.dma_start(
+                tab2_sc[32 * q : 32 * q + 8, :].bitcast(I32), tab2_scales[:, 4 * q : 4 * q + 4, :].bitcast(I32)
+            )
+        pos1_t = load_list(pos1, "pos1_t")
+        pos2_t = load_list(pos2, "pos2_t")
+        w_raw[0, 1] = load_w1(0, 1)
+        w_raw[1, 1] = load_w1(1, 1)
+        prop_t = keep.tile([P, ROW_TILES], F32, name="prop_t")
+        with nc.allow_non_contiguous_dma(reason="one value of prop for each row of out"):
+            nc.sync.dma_start(prop_t[:], prop.rearrange("(j p) -> p j", p=P))
+        tab2_w = [load_words(tab2_words, b, f"tab2_w{b}") for b in range(PASSES)]
+
+        tab_sc = sbuf([P, T], U8, "tab_sc")
+        nc.vector.memset(tab_sc[:].bitcast(I32), 0)
+        for q in range(4):
+            rows = slice(32 * q, 32 * q + 8)
+            nc.vector.tensor_copy(tab_sc[rows, :].bitcast(I32), landed[rows, :].bitcast(I32))
+
+        wq = {(a, 0): quantize(round_w1(w_raw[a, 0], True, f"w_bf{a}0"), f"wq{a}0") for a in range(PASSES)}
+
+        gain_rows = {}
+        for b in range(PASSES):
+            for t in range(PACK):
+                gain_rows[b, t] = keep.tile([P, OUTFITS], F32, name=f"gain_rows{b}{t}")
+                nc.scalar.activation(gain_rows[b, t][:], gain_t[:, b, t : t + 1].to_broadcast([P, OUTFITS]), ACT.Copy)
+
+        v_sc = sbuf([P, S], U8, "v_sc")
+        nc.vector.tensor_copy(v_sc[:], looked_up(tab_sc[:], offs_t, 0, S))
+        v_w = [sbuf([P, S], U32, "v_w0", "tab_sc"), sbuf([P, S], U32, "v_w1")]
+        nc.vector.tensor_copy(v_w[0][:], looked_up(tab_w[0][:].bitcast(U32), offs_t, 0, S))
+        lo = 0
+        for width in FIRST_PIECES:
+            nc.vector.tensor_copy(
+                v_w[1][:, lo : lo + width], looked_up(tab_w[1][:].bitcast(U32), offs_t, lo, lo + width)
+            )
+            lo += width
+
+        v2_sc = sbuf([P, S2], U8, "v2_sc", "tab_w1")
+        nc.vector.tensor_copy(v2_sc[:], looked_up(tab2_sc[:], offs2_t, 0, S2))
+
+        def first_products(b, t, widths, bank_ids):
+            pieces = []
+            lo = 0
+            for width, i in zip(widths, bank_ids):
+                pieces.append((bank(i, [P, width]), slice(lo, lo + width)))
+                lo += width
+            for a in range(PASSES):
+                codes, scales = wq[a, b]
+                for acc, cols in pieces:
+                    nc.tensor.matmul_mx(
+                        out=acc[:],
+                        lhsT=codes[:, P * t : P * (t + 1)].bitcast(FP8X4),
+                        lhsT_scale=scales[:, P * t : P * (t + 1)],
+                        rhs=v_w[a][:, cols].bitcast(FP8X4),
+                        rhs_scale=v_sc[4 * a : P, cols],
+                        start=(a == 0),
+                        stop=(a == PASSES - 1),
+                    )
+            return pieces
+
+        def two_banks(b, t):
+            return first_products(b, t, [BANK, BANK], [2 * t, 2 * t + 1])
+
+        def features(b, t, pieces, tag=None):
+            tile = sbuf([P, S], F32, f"h{b}{t}", tag)
+            for acc, cols in pieces:
+                nc.scalar.activation(tile[:, cols], acc[:], ACT.Tanh, bias=b1_t[:, b, t : t + 1])
+            return tile
+
+        def pick(dst, b, t, offsets, lo, hi):
+            nc.vector.tensor_tensor(
+                dst, looked_up(h[b, t][:], offsets, lo, hi), gain_rows[b, t][:, 0 : hi - lo], ALU.mult
+            )
+
         h = {}
-        for t in range(PACK):
-            h[0, t] = first_stage(0, t, LAST_GATHER if t == 0 else [BANK, BANK])
+        sums = [first_products(0, 0, FIRST_PIECES, [0, 1, 7])]
+        h[0, 0] = features(0, 0, sums[0])
+        sums.extend(two_banks(0, t) for t in range(1, PACK))
+        h[0, 1] = features(0, 1, sums[1])
+        lead = [sbuf([P, PACK, OUTFITS], F32, "lead0")]
+        accent0 = sbuf([P, PACK, OUTFITS], F32, "accent0")
+        for t in range(2):
+            pick(lead[0][:, t, :], 0, t, pos1_t, 0, OUTFITS)
+            pick(accent0[:, t, :], 0, t, pos2_t, 0, OUTFITS)
+        wq[0, 1] = quantize(round_w1(w_raw[0, 1], False, "wq10_codes"), "wq01")
+        wq[1, 1] = quantize(round_w1(w_raw[1, 1], False, "wq10_scales"), "wq11")
+        h[0, 2] = features(0, 2, sums[2], "w_raw11")
+        h[0, 3] = features(0, 3, sums[3], "wq10_scales")
+        for t in range(2, PACK):
+            pick(lead[0][:, t, :], 0, t, pos1_t, 0, OUTFITS)
+            pick(accent0[:, t, :], 0, t, pos2_t, 0, OUTFITS)
 
-        w01_bf = round_w1(w_raw[0, 1], True, "tab_w1")
-
-        lead = keep.tile([P, PACK, NP], F32, name="lead0", tag="slot_e", align_bytes=64)
         for t in range(PACK):
-            pick(lead[:, t, :], 0, t, h[0, t], pos1_t, 0, NP)
-        wq[0, 1] = quantize(w01_bf, "wq01")
-        v2_sc = keep.tile([P, S2], U8, name="v2_sc", align_bytes=64)
-        gather(v2_sc[:], tab2_sc[:], offs2_t, 0, S2)
-        wq[1, 1] = quantize(round_w1(w_raw[1, 1], False, "slot_d"), "wq11", ("slot_a", "slot_b"))
-        accent = keep.tile([P, PACK, NP], F32, name="accent0", tag="slot_d", align_bytes=64)
-        for t in range(PACK):
-            pick(accent[:, t, :], 0, t, h[0, t], pos2_t, 0, NP)
-        for t in range(PACK):
-            h[1, t] = first_stage(1, t, [BANK, BANK])
+            h[1, t] = features(1, t, two_banks(1, t))
 
-        v2_w = [keep.tile([P, S2], U32, name=f"v2_w{b}", align_bytes=64) for b in range(2)]
-        for b in range(2):
-            gather(v2_w[b][:], tab2_w[b][:].bitcast(U32), offs2_t, 0, S2)
+        v2_w = [sbuf([P, S2], U32, f"v2_w{b}") for b in range(PASSES)]
+        for b in range(PASSES):
+            nc.vector.tensor_copy(v2_w[b][:], looked_up(tab2_w[b][:].bitcast(U32), offs2_t, 0, S2))
 
-        x1_bf0 = round_x(lead, ACT.Copy, "slot_c")
-        x2_bf0 = round_x(accent, ACT.Abs, "slot_b")
-        lead = keep.tile([P, PACK, NP], F32, name="lead1", tag="slot_f", align_bytes=64)
-        for t in range(PACK):
-            pick(lead[:, t, :], 1, t, h[1, t], pos1_t, 0, NP)
-            if t == 1:
-                x1q0 = quantize(x1_bf0, "x1q0")
-            if t == 3:
-                x2q0 = quantize(x2_bf0, "x2q0")
-        x1_bf1 = round_x(lead, ACT.Copy, "slot_g")
+        x1_bf0 = round_x(lead[0], ACT.Copy, "wq11_codes")
+        x2_bf0 = round_x(accent0, ACT.Abs, "wq11_scales")
+        lead.append(sbuf([P, PACK, OUTFITS], F32, "lead1"))
+        for t in range(2):
+            pick(lead[1][:, t, :], 1, t, pos1_t, 0, OUTFITS)
+        x1q = [quantize(x1_bf0, "x1q0")]
+        for t in range(2, PACK):
+            pick(lead[1][:, t, :], 1, t, pos1_t, 0, OUTFITS)
+        x2q0 = quantize(x2_bf0, "x2q0")
+        x1_bf1 = round_x(lead[1], ACT.Copy, "x1_bf1")
 
-        def second_stage(dst, b, j, xq, lo, hi, start, stop):
+        def second_product(dst, b, j, xq, lo, hi, start, stop):
             codes, scales = xq
             nc.tensor.matmul_mx(
                 out=dst,
@@ -240,41 +232,42 @@ def tile_list_window_outfit_scorer_kernel(
                 stop=stop,
             )
 
-        e1 = [bank(j, [P, NP]) for j in range(4)]
-        for j in range(4):
-            second_stage(e1[j][:], 0, j, x1q0, 0, NP, True, False)
-        e2 = []
-        lo = 0
-        nbank = 4
-        for width in TAIL:
-            per = BANK // width
-            for j0 in range(0, 4, per):
-                tile = bank(nbank, [P, per, width])
-                nbank += 1
-                for i in range(per):
-                    second_stage(tile[:, i, :], 0, j0 + i, x2q0, lo, lo + width, i == 0, False)
-                e2.append((tile, j0, per, lo, width))
-            lo += width
+        e1 = [bank(j, [P, OUTFITS]) for j in range(ROW_TILES)]
+        for j in range(ROW_TILES):
+            second_product(e1[j][:], 0, j, x1q[0], 0, OUTFITS, True, False)
+        per_bank = BANK // SLICE
+        parts = [(lo, j0) for lo in range(0, OUTFITS, SLICE) for j0 in range(0, ROW_TILES, per_bank)]
+        e2 = {}
+        for n, (lo, j0) in enumerate(parts):
+            e2[lo, j0] = bank(ROW_TILES + n, [P, per_bank, SLICE])
+            for i in range(per_bank):
+                second_product(e2[lo, j0][:, i, :], 0, j0 + i, x2q0, lo, lo + SLICE, i == 0, False)
 
-        weighed = keep.tile([P, 4, NP], F32, name="weighed")
-        out_v = out.rearrange("(j p) n -> p j n", p=P)
-        lo = 0
-        for s, width in enumerate(TAIL):
-            accent = keep.tile([P, PACK, width], F32, name="accent1", tag=("slot_e", "slot_f", "slot_g")[s], align_bytes=64)
+        def pick_accent(lo, tag):
+            tile = sbuf([P, PACK, SLICE], F32, "accent1", tag)
             for t in range(PACK):
-                pick(accent[:, t, :], 1, t, h[1, t], pos2_t, lo, lo + width)
-                if s == 0 and t == 2:
-                    x1q1 = quantize(x1_bf1, "x1q1")
-                    for j in range(4):
-                        second_stage(e1[j][:], 1, j, x1q1, 0, NP, False, True)
-                        nc.scalar.activation(weighed[:, j, :], e1[j][:], ACT.Copy, scale=prop_t[:, j : j + 1])
-            xq = quantize(round_x(accent, ACT.Abs, f"x2_bf1{s}"), f"x2q1{s}")
-            for tile, j0, per, lo2, width2 in e2:
-                if lo2 == lo:
-                    for i in range(per):
-                        second_stage(tile[:, i, :], 1, j0 + i, xq, 0, width, False, i == per - 1)
-            lo += width
-        for tile, j0, per, lo, width in e2:
-            res = ring.tile([P, per, width], F32, name="res", bufs=4)
-            nc.vector.tensor_tensor(res[:], tile[:], weighed[:, j0 : j0 + per, lo : lo + width], ALU.add)
-            nc.sync.dma_start(out_v[:, j0 : j0 + per, lo : lo + width], res[:])
+                pick(tile[:, t, :], 1, t, pos2_t, lo, lo + SLICE)
+            return tile
+
+        def finish_accent(picked, lo, tag):
+            xq = quantize(round_x(picked, ACT.Abs, tag), f"x2q1_{lo}")
+            for j in range(ROW_TILES):
+                i = j % per_bank
+                second_product(e2[lo, j - i][:, i, :], 1, j, xq, 0, SLICE, False, i == per_bank - 1)
+
+        first_slice = pick_accent(0, "accent0")
+        x1q.append(quantize(x1_bf1, "x1q1"))
+        weighed = keep.tile([P, ROW_TILES, OUTFITS], F32, name="weighed")
+        for j in range(ROW_TILES):
+            second_product(e1[j][:], 1, j, x1q[1], 0, OUTFITS, False, True)
+            nc.scalar.activation(weighed[:, j, :], e1[j][:], ACT.Copy, scale=prop_t[:, j : j + 1])
+        finish_accent(first_slice, 0, "x2_bf1")
+        finish_accent(pick_accent(SLICE, "x1_bf1"), SLICE, "x1q1_codes")
+
+        out_rows = out.rearrange("(j p) n -> p j n", p=P)
+        for lo, j0 in parts:
+            result = keep.tile([P, per_bank, SLICE], F32, name=f"result{lo}_{j0}")
+            nc.vector.tensor_tensor(
+                result[:], e2[lo, j0][:], weighed[:, j0 : j0 + per_bank, lo : lo + SLICE], ALU.add
+            )
+            nc.sync.dma_start(out_rows[:, j0 : j0 + per_bank, lo : lo + SLICE], result[:])

@@ -96,7 +96,7 @@ def tile_list_window_outfit_scorer_kernel(
             row = 32 * q + 4 * a
             nc.sync.dma_start(landed[row : row + 4, :].bitcast(I32), tab_scales[a, 4 * q : 4 * q + 4, :].bitcast(I32))
 
-        runs = [(a, q) for q in range(4) for a in range(PASSES)]
+        runs = [(a, q) for q in (0, 2, 1, 3) for a in range(PASSES)]
         for a, q in runs[:-1]:
             load_scale_rows(a, q)
         w_raw = {(0, 0): load_w1(0, 0)}

from contextlib import ExitStack

import concourse.mybir as mybir

F32 = mybir.dt.float32
BF16 = mybir.dt.bfloat16
I32 = mybir.dt.int32
U32 = mybir.dt.uint32
U16 = mybir.dt.uint16
U8 = mybir.dt.uint8
FP8X4 = mybir.dt.float8_e4m3fn_x4
ACT = mybir.ActivationFunctionType
ALU = mybir.AluOpType

P = 128
PACK = 4
K_PASS = P * PACK
PASSES = 2
BANK = 512
K, H, T, S, S2, OUTFITS = 1024, 1024, 4096, 1024, 512, 512
ROW_TILES = S2 // P
FLOPS = 2 * K * H * S + 2 * 2 * H * S2 * OUTFITS

FIRST_PIECES = [512, 256, 256]
SLICE = 256


def tile_list_window_outfit_scorer_kernel(
    tc, tab_words, tab_scales, offs, tab2_words, tab2_scales, offs2, pos1, pos2, w1, b1, gain, prop, out
):
    nc = tc.nc
    with ExitStack() as ctx:
        lists = ctx.enter_context(tc.tile_pool(name="lists", bufs=1))
        keep = ctx.enter_context(tc.tile_pool(name="keep", bufs=1))
        psum = ctx.enter_context(tc.psum_pool(name="psum", bufs=1))

        def sbuf(shape, dtype, name, tag=None):
            return keep.tile(shape, dtype, name=name, tag=tag or name, align_bytes=64)

        def bank(i, shape):
            return psum.tile(shape, F32, name=f"bank{i}")

        def load_list(src, name):
            tile = lists.tile([P, src.shape[1]], U16, name=name)
            nc.sync.dma_start(tile[:], src)
            return tile

        def load_words(words, a, name):
            tile = sbuf([P, words.shape[2]], I32, name)
            nc.sync.dma_start(tile[:], words[a].rearrange("p n i -> p (n i)").bitcast(I32))
            return tile

        def load_w1(a, b):
            tile = sbuf([P, PACK, K_PASS], F32, f"w_raw{a}{b}")
            src = w1[K_PASS * a : K_PASS * (a + 1), K_PASS * b : K_PASS * (b + 1)]
            nc.sync.dma_start(tile[:], src.rearrange("(p j) c -> p j c", j=PACK))
            return tile

        def load_per_row(vector, name):
            tile = keep.tile([P, PASSES, PACK], F32, name=name)
            nc.sync.dma_start(tile[:], vector.rearrange("(b p t) -> p b t", b=PASSES, t=PACK))
            return tile

        def round_w1(raw, on_vector, tag):
            tile = sbuf([P, PACK, P, PACK], BF16, "w_bf", tag)
            dst = tile[:].rearrange("p t m j -> p m j t")
            src = raw[:].rearrange("p j (m t) -> p m j t", t=PACK)
            if on_vector:
                nc.vector.tensor_copy(dst, src)
            else:
                nc.scalar.activation(dst, src, ACT.Copy)
            return tile[:].rearrange("p t m j -> p (t m j)")

        def round_x(picked, func, tag):
            tile = sbuf([P, picked.shape[2], PACK], BF16, "x_bf", tag)
            nc.scalar.activation(
                tile[:].rearrange("p (c i) t -> p c t i", i=4),
                picked[:].rearrange("p t (c i) -> p c t i", i=4),
                func,
            )
            return tile[:].rearrange("p n t -> p (n t)")

        def quantize(values, name):
            width = values.shape[1] // PACK
            codes = sbuf([P, width], U32, name + "_codes")
            scales = sbuf([P, width], U8, name + "_scales")
            nc.vector.quantize_mx(out=codes[:].bitcast(FP8X4), scales=scales[:], in_=values)
            return codes, scales

        def looked_up(window, offsets, lo, hi):
            return window.indirect(offsets[:, lo // 16 : hi // 16])

        landed = sbuf([P, T], U8, "landed")

        def load_scale_rows(a, q):
            row = 32 * q + 4 * a
            nc.sync.dma_start(landed[row : row + 4, :].bitcast(I32), tab_scales[a, 4 * q : 4 * q + 4, :].bitcast(I32))

        runs = [(a, q) for q in (0, 2, 1, 3) for a in range(PASSES)]
        for a, q in runs[:-1]:
            load_scale_rows(a, q)
        w_raw = {(0, 0): load_w1(0, 0)}
        load_scale_rows(*runs[-1])
        offs_t = load_list(offs, "offs_t")
        gain_t = load_per_row(gain, "gain_t")
        b1_t = load_per_row(b1, "b1_t")
        w_raw[1, 0] = load_w1(1, 0)
        tab_w = [load_words(tab_words, a, f"tab_w{a}") for a in range(PASSES)]
        offs2_t = load_list(offs2, "offs2_t")
        tab2_sc = sbuf([P, tab2_scales.shape[2]], U8, "tab2_sc")
        nc.vector.memset(tab2_sc[:].bitcast(I32), 0)
        for q in range(4):
            nc.sync.dma_start(
                tab2_sc[32 * q : 32 * q + 8, :].bitcast(I32), tab2_scales[:, 4 * q : 4 * q + 4, :].bitcast(I32)
            )
        pos1_t = load_list(pos1, "pos1_t")
        pos2_t = load_list(pos2, "pos2_t")
        w_raw[0, 1] = load_w1(0, 1)
        w_raw[1, 1] = load_w1(1, 1)
        prop_t = keep.tile([P, ROW_TILES], F32, name="prop_t")
        with nc.allow_non_contiguous_dma(reason="one value of prop for each row of out"):
            nc.sync.dma_start(prop_t[:], prop.rearrange("(j p) -> p j", p=P))
        tab2_w = [load_words(tab2_words, b, f"tab2_w{b}") for b in range(PASSES)]

        tab_sc = sbuf([P, T], U8, "tab_sc")
        nc.vector.memset(tab_sc[:].bitcast(I32), 0)
        for q in range(4):
            rows = slice(32 * q, 32 * q + 8)
            nc.vector.tensor_copy(tab_sc[rows, :].bitcast(I32), landed[rows, :].bitcast(I32))

        wq = {(a, 0): quantize(round_w1(w_raw[a, 0], True, f"w_bf{a}0"), f"wq{a}0") for a in range(PASSES)}

        gain_rows = {}
        for b in range(PASSES):
            for t in range(PACK):
                gain_rows[b, t] = keep.tile([P, OUTFITS], F32, name=f"gain_rows{b}{t}")
                nc.scalar.activation(gain_rows[b, t][:], gain_t[:, b, t : t + 1].to_broadcast([P, OUTFITS]), ACT.Copy)

        v_sc = sbuf([P, S], U8, "v_sc")
        nc.vector.tensor_copy(v_sc[:], looked_up(tab_sc[:], offs_t, 0, S))
        v_w = [sbuf([P, S], U32, "v_w0", "tab_sc"), sbuf([P, S], U32, "v_w1")]
        nc.vector.tensor_copy(v_w[0][:], looked_up(tab_w[0][:].bitcast(U32), offs_t, 0, S))
        lo = 0
        for width in FIRST_PIECES:
            nc.vector.tensor_copy(
                v_w[1][:, lo : lo + width], looked_up(tab_w[1][:].bitcast(U32), offs_t, lo, lo + width)
            )
            lo += width

        v2_sc = sbuf([P, S2], U8, "v2_sc", "tab_w1")
        nc.vector.tensor_copy(v2_sc[:], looked_up(tab2_sc[:], offs2_t, 0, S2))

        def first_products(b, t, widths, bank_ids):
            pieces = []
            lo = 0
            for width, i in zip(widths, bank_ids):
                pieces.append((bank(i, [P, width]), slice(lo, lo + width)))
                lo += width
            for a in range(PASSES):
                codes, scales = wq[a, b]
                for acc, cols in pieces:
                    nc.tensor.matmul_mx(
                        out=acc[:],
                        lhsT=codes[:, P * t : P * (t + 1)].bitcast(FP8X4),
                        lhsT_scale=scales[:, P * t : P * (t + 1)],
                        rhs=v_w[a][:, cols].bitcast(FP8X4),
                        rhs_scale=v_sc[4 * a : P, cols],
                        start=(a == 0),
                        stop=(a == PASSES - 1),
                    )
            return pieces

        def two_banks(b, t):
            return first_products(b, t, [BANK, BANK], [2 * t, 2 * t + 1])

        def features(b, t, pieces, tag=None):
            tile = sbuf([P, S], F32, f"h{b}{t}", tag)
            for acc, cols in pieces:
                nc.scalar.activation(tile[:, cols], acc[:], ACT.Tanh, bias=b1_t[:, b, t : t + 1])
            return tile

        def pick(dst, b, t, offsets, lo, hi):
            nc.vector.tensor_tensor(
                dst, looked_up(h[b, t][:], offsets, lo, hi), gain_rows[b, t][:, 0 : hi - lo], ALU.mult
            )

        h = {}
        sums = [first_products(0, 0, FIRST_PIECES, [0, 1, 7])]
        h[0, 0] = features(0, 0, sums[0])
        sums.extend(two_banks(0, t) for t in range(1, PACK))
        h[0, 1] = features(0, 1, sums[1])
        lead = [sbuf([P, PACK, OUTFITS], F32, "lead0")]
        accent0 = sbuf([P, PACK, OUTFITS], F32, "accent0")
        for t in range(2):
            pick(lead[0][:, t, :], 0, t, pos1_t, 0, OUTFITS)
            pick(accent0[:, t, :], 0, t, pos2_t, 0, OUTFITS)
        wq[0, 1] = quantize(round_w1(w_raw[0, 1], False, "wq10_codes"), "wq01")
        wq[1, 1] = quantize(round_w1(w_raw[1, 1], False, "wq10_scales"), "wq11")
        h[0, 2] = features(0, 2, sums[2], "w_raw11")
        h[0, 3] = features(0, 3, sums[3], "wq10_scales")
        for t in range(2, PACK):
            pick(lead[0][:, t, :], 0, t, pos1_t, 0, OUTFITS)
            pick(accent0[:, t, :], 0, t, pos2_t, 0, OUTFITS)

        for t in range(PACK):
            h[1, t] = features(1, t, two_banks(1, t))

        v2_w = [sbuf([P, S2], U32, f"v2_w{b}") for b in range(PASSES)]
        for b in range(PASSES):
            nc.vector.tensor_copy(v2_w[b][:], looked_up(tab2_w[b][:].bitcast(U32), offs2_t, 0, S2))

        x1_bf0 = round_x(lead[0], ACT.Copy, "wq11_codes")
        x2_bf0 = round_x(accent0, ACT.Abs, "wq11_scales")
        lead.append(sbuf([P, PACK, OUTFITS], F32, "lead1"))
        for t in range(2):
            pick(lead[1][:, t, :], 1, t, pos1_t, 0, OUTFITS)
        x1q = [quantize(x1_bf0, "x1q0")]
        for t in range(2, PACK):
            pick(lead[1][:, t, :], 1, t, pos1_t, 0, OUTFITS)
        x2q0 = quantize(x2_bf0, "x2q0")
        x1_bf1 = round_x(lead[1], ACT.Copy, "x1_bf1")

        def second_product(dst, b, j, xq, lo, hi, start, stop):
            codes, scales = xq
            nc.tensor.matmul_mx(
                out=dst,
                lhsT=v2_w[b][:, P * j : P * (j + 1)].bitcast(FP8X4),
                lhsT_scale=v2_sc[4 * b : P, P * j : P * (j + 1)],
                rhs=codes[:, lo:hi].bitcast(FP8X4),
                rhs_scale=scales[:, lo:hi],
                start=start,
                stop=stop,
            )

        e1 = [bank(j, [P, OUTFITS]) for j in range(ROW_TILES)]
        for j in range(ROW_TILES):
            second_product(e1[j][:], 0, j, x1q[0], 0, OUTFITS, True, False)
        per_bank = BANK // SLICE
        parts = [(lo, j0) for lo in range(0, OUTFITS, SLICE) for j0 in range(0, ROW_TILES, per_bank)]
        e2 = {}
        for n, (lo, j0) in enumerate(parts):
            e2[lo, j0] = bank(ROW_TILES + n, [P, per_bank, SLICE])
            for i in range(per_bank):
                second_product(e2[lo, j0][:, i, :], 0, j0 + i, x2q0, lo, lo + SLICE, i == 0, False)

        def pick_accent(lo, tag):
            tile = sbuf([P, PACK, SLICE], F32, "accent1", tag)
            for t in range(PACK):
                pick(tile[:, t, :], 1, t, pos2_t, lo, lo + SLICE)
            return tile

        def finish_accent(picked, lo, tag):
            xq = quantize(round_x(picked, ACT.Abs, tag), f"x2q1_{lo}")
            for j in range(ROW_TILES):
                i = j % per_bank
                second_product(e2[lo, j - i][:, i, :], 1, j, xq, 0, SLICE, False, i == per_bank - 1)

        first_slice = pick_accent(0, "accent0")
        x1q.append(quantize(x1_bf1, "x1q1"))
        weighed = keep.tile([P, ROW_TILES, OUTFITS], F32, name="weighed")
        for j in range(ROW_TILES):
            second_product(e1[j][:], 1, j, x1q[1], 0, OUTFITS, False, True)
            nc.scalar.activation(weighed[:, j, :], e1[j][:], ACT.Copy, scale=prop_t[:, j : j + 1])
        finish_accent(first_slice, 0, "x2_bf1")
        finish_accent(pick_accent(SLICE, "x1_bf1"), SLICE, "x1q1_codes")

        out_rows = out.rearrange("(j p) n -> p j n", p=P)
        for lo, j0 in parts:
            result = keep.tile([P, per_bank, SLICE], F32, name=f"result{lo}_{j0}")
            nc.vector.tensor_tensor(
                result[:], e2[lo, j0][:], weighed[:, j0 : j0 + per_bank, lo : lo + SLICE], ALU.add
            )
            nc.sync.dma_start(out_rows[:, j0 : j0 + per_bank, lo : lo + SLICE], result[:])
